import numpy as np
import ml_dtypes


def mxq(x, axis, fmt="e4m3"):
    dtype, down = {"e4m3": (ml_dtypes.float8_e4m3fn, 7), "e5m2": (ml_dtypes.float8_e5m2, 14)}[fmt]
    v = np.moveaxis(np.asarray(x, np.float32).astype(ml_dtypes.bfloat16).astype(np.float64), axis, -1)
    blocks = v.reshape(v.shape[:-1] + (-1, 32))
    amax = np.abs(blocks).max(-1, keepdims=True)
    byte = np.maximum(np.where(amax > 0, np.frexp(amax)[1] - 1 + 127, 0) - down, 1)
    scale = np.exp2(byte - 127.0)
    codes = (blocks / scale).astype(np.float32).astype(dtype).astype(np.float64)
    return np.moveaxis((codes * scale).reshape(v.shape), -1, axis)


WIDE = False


def mx_kscale(k):
    if not WIDE:
        return np.ones(k)
    levels = np.array([10, -10, 5, -5, 0])
    if k % 512:
        return np.exp2(np.random.permutation(np.resize(levels, k // 32))).repeat(32)
    a = np.empty((k // 512, 16))
    for p in range(k // 512):
        a[p, :8] = np.random.permutation(np.resize(levels, 8))
        for g in range(8):
            far = levels[np.abs(levels - a[p, g]) >= 10]
            a[p, g + 8] = far[np.random.randint(len(far))]
    return np.exp2(a.ravel()).repeat(32)


BF16 = ml_dtypes.bfloat16


def bf(x):
    return np.asarray(x, np.float32).astype(BF16)


def f64(x):
    return np.asarray(x).astype(np.float64)


E2M1 = np.array([0.0, 0.5, 1.0, 1.5, 2.0, 3.0, 4.0, 6.0, -0.0, -0.5, -1.0, -1.5, -2.0, -3.0, -4.0, -6.0])


def pack_weight(w, fmt):
    k, n = w.shape
    w = f64(bf(w)).reshape(k // 32, 32, n)
    amax = np.abs(w).max(1)
    if fmt == "e4m3":
        byte = np.frexp(amax)[1] - 1 + 127 - 7
    else:
        mant, ex = np.frexp(amax / 6.0)
        byte = np.where(mant > 0.5, ex, ex - 1) + 127
    byte = np.clip(np.where(amax > 0, byte, 1), 1, 254)
    scaled = (w * np.exp2(127.0 - byte)[:, None, :]).reshape(k, n).astype(np.float32)
    by_word = np.ascontiguousarray(scaled.reshape(k // 512, 128, 4, n).transpose(0, 1, 3, 2))
    if fmt == "e4m3":
        words = by_word.astype(ml_dtypes.float8_e4m3fn).view(np.uint8)
    else:
        c = by_word.astype(ml_dtypes.float4_e2m1fn).view(np.uint8) & 0xF
        words = c[..., 0::2] | (c[..., 1::2] << 4)
    return np.ascontiguousarray(words), np.ascontiguousarray(byte.astype(np.uint8).reshape(k // 512, 16, n))


def unpack_weight(words, scales, fmt):
    g, p, n, _ = words.shape
    if fmt == "e4m3":
        vals = np.ascontiguousarray(words).view(ml_dtypes.float8_e4m3fn).astype(np.float64)
    else:
        nib = np.empty((g, p, n, 4), np.uint8)
        nib[..., 0::2] = words & 0xF
        nib[..., 1::2] = words >> 4
        vals = E2M1[nib]
    vals = vals * np.repeat(np.exp2(scales.astype(np.float64) - 127.0), 8, axis=1)[..., None]
    return vals.transpose(0, 1, 3, 2).reshape(g * 512, n)
def pack4(w):
    words, scales = pack_weight(w, "e2m1")
    return words.reshape(words.shape[0], 128, -1), scales


def unpack4(words, scales):
    return unpack_weight(words.reshape(words.shape[0], 128, -1, 2), scales, "e2m1")


def planes(Y):
    n, m = Y.shape
    b = f64(bf(Y)).reshape(n // 32, 32, m)
    amax = np.abs(b).max(1)
    byte = np.clip(np.where(amax > 0, np.frexp(amax)[1] - 1 + 127 - 7, 1), 1, 254)
    codes = (b * np.exp2(127.0 - byte)[:, None, :]).reshape(n, m).astype(np.float32).astype(ml_dtypes.float8_e4m3fn).view(np.uint8)
    words = codes.reshape(n // 512, 128, 4, m).transpose(0, 1, 3, 2)
    return np.ascontiguousarray(words), np.ascontiguousarray(byte.astype(np.uint8).reshape(n // 512, 16, m))


S, C, L, H = 1024, 1536, 1024, 512

def noise(*shape):
    return np.random.standard_normal(shape)

def setup_inputs():
    v, u, t = mx_kscale(S), mx_kscale(L), mx_kscale(L)
    series_words, series_scales = pack_weight(noise(S, L) * v[:, None], "e4m3")
    lag = np.abs(np.arange(L)[:, None] - np.arange(L)[None, :]) / L
    avg = np.exp(-4.0 * lag + 0.5 * noise(L, L))
    avg = avg / avg.sum(axis=0, keepdims=True)
    diff_words, diff_scales = pack4(0.75 * noise(L, H) / u[:, None])
    return {
        "series_words": series_words, "series_scales": series_scales,
        "mix": bf(noise(S, C) / np.sqrt(S) / v[:, None]),
        "time_gain": bf(np.exp(0.3 * noise(L)) * t),
        "avg": bf(avg / t[:, None] * u[None, :]),
        "diff_words": diff_words, "diff_scales": diff_scales,
        "w_rem": bf(noise(L, H) / np.sqrt(L) / t[:, None]),
        "h_bias": bf(0.5 * noise(H)),
        "ch_scale": bf(0.7 * np.exp(0.8 * noise(C))),
        "ch_level": bf(0.3 * noise(C)),
    }

def reference(series_words, series_scales, mix, time_gain, avg, diff_words, diff_scales, w_rem, h_bias, ch_scale, ch_level):
    X = (mxq(f64(mix), 0).T @ unpack_weight(series_words, series_scales, "e4m3")) * f64(time_gain)[None, :]
    V = (mxq(f64(avg), 1) @ unpack4(diff_words, diff_scales)) + f64(w_rem)
    y = mxq(X, 1) @ mxq(V, 0)
    y = (y + f64(h_bias)[None, :]) * f64(ch_scale)[:, None] + f64(ch_level)[:, None]
    Y = y
    words, scales = planes(Y)
    return y, words, scales

@@ -1,0 +1,414 @@
+from contextlib import ExitStack
+
+import concourse.mybir as mybir
+from concourse.masks import make_identity
+
+S, C, L, H = 1024, 1536, 1024, 512
+FLOPS = 2 * (S * C * L + L * L * H + C * L * H)
+
+F32 = mybir.dt.float32
+BF16 = mybir.dt.bfloat16
+I32 = mybir.dt.int32
+U32 = mybir.dt.uint32
+U8 = mybir.dt.uint8
+FP8X4 = mybir.dt.float8_e4m3fn_x4
+FP4X4 = mybir.dt.float4_e2m1fn_x4
+ALU = mybir.AluOpType
+ACT = mybir.ActivationFunctionType
+
+P = 128
+PACK = 4
+KP = P * PACK
+NG = C // KP
+RUN = 4
+
+
+def tile_merged_dlinear_style_forecast_k4_kernel(
+    tc, series_words, series_scales, mix, time_gain, avg, diff_words, diff_scales, w_rem, h_bias, ch_scale, ch_level,
+    out_0, out_1, out_2,
+):
+    nc = tc.nc
+    with ExitStack() as ctx:
+        keep = ctx.enter_context(tc.tile_pool(name="keep", bufs=1))
+        psum = ctx.enter_context(tc.psum_pool(name="psum", bufs=8))
+        ctx.enter_context(tc.manual_schedule())
+
+        def sb(name, shape, dtype, tag=None, bufs=1):
+            return keep.tile(shape, dtype, name=name, tag=tag or name, bufs=bufs, align_bytes=64)
+
+        def bank(name, shape, dtype=F32):
+            return psum.tile(shape, dtype, name=name, tag="bank")
+
+        def interleave(engine, dst, src, lo, hi):
+            out = dst[:, lo:hi, :].rearrange("p (c i) t -> p c t i", i=RUN)
+            in_ = src[:, :, lo:hi].rearrange("p t (c i) -> p c t i", i=RUN)
+            if engine == "vector":
+                nc.vector.tensor_copy(out=out, in_=in_)
+            else:
+                nc.scalar.copy(out=out, in_=in_)
+
+        def quantize(codes, scales, grouped):
+            nc.vector.quantize_mx(out=codes.bitcast(FP8X4), scales=scales, in_=grouped.rearrange("p c t -> p (c t)"))
+
+        ident = sb("ident", [P, P], F32)
+        ident_bf = sb("ident_bf", [P, P], BF16)
+        zs_raw = sb("zs_raw", [P, 2, L], U8)
+        zs = sb("zs", [P, 2, L], U8)
+        ds = sb("ds", [P, 2, H], U8)
+        dw = sb("dw", [P, 2, 2 * H], U8)
+        gain_rows = sb("gain_rows", [P, P], BF16)
+        gain = sb("gain", [P, 2 * PACK], F32)
+        hb_words = sb("hb_words", [P, PACK], BF16)
+        hb_all = sb("hb_all", [P, H], BF16)
+        ch_raw = sb("ch_raw", [P, 2, 16], BF16)
+        ch = sb("ch", [P, 2, NG * PACK], F32)
+        y_scales = sb("y_scales", [P, NG, H], U8)
+
+        p_raw, p_grp, p_codes, p_scales = {}, {}, {}, {}
+        z_raw, z_codes = {}, {}
+        a_raw, a_grp, a_codes, a_scales = {}, {}, {}, {}
+        r_raw, v_grp, v_codes, v_scales = {}, {}, {}, {}
+        x_slots, x_grp, x_codes, x_scales = {}, {}, {}, {}
+        offset, y32, y_grp, y_codes = {}, {}, {}, {}
+
+        def load_p(G, g, lo=0, hi=KP):
+            if lo == 0:
+                p_raw[G, g] = sb("p_raw%d%d" % (G, g), [P, PACK, KP], BF16, tag="p_raw", bufs=4)
+            src = mix[g * KP : (g + 1) * KP, G * KP + lo : G * KP + hi].rearrange("(p j) c -> p j c", j=PACK)
+            nc.sync.dma_start(out=p_raw[G, g][:, :, lo:hi], in_=src)
+
+        def load_z(gl):
+            z_raw[gl] = sb("z_raw%d" % gl, [P, 2, KP], U32)
+            src = series_words.rearrange("g p n t -> p g (n t)")[:, :, gl * KP * 4 : (gl + 1) * KP * 4].bitcast(I32)
+            nc.sync.dma_start(out=z_raw[gl][:].bitcast(I32), in_=src)
+
+        def load_plane(queue, plane, rows):
+            for q in range(4):
+                src = rows[:, 4 * q : 4 * q + 4, :].rearrange("g r n -> r g n").bitcast(I32)
+                queue.dma_start(out=plane[32 * q : 32 * q + 4, :, :].bitcast(I32), in_=src)
+
+        def load_a(gl, gj):
+            a_raw[gl, gj] = sb("a_raw%d%d" % (gl, gj), [P, PACK, KP], BF16)
+            src = avg[gl * KP : (gl + 1) * KP, gj * KP : (gj + 1) * KP].rearrange("(a p) j -> p a j", p=P)
+            nc.sync.dma_start(out=a_raw[gl, gj][:], in_=src)
+
+        def load_d():
+            load_plane(nc.sync, ds, diff_scales)
+            nc.sync.dma_start(out=dw[:].bitcast(I32), in_=diff_words.rearrange("g p n -> p g n").bitcast(I32))
+
+        def load_r(gl):
+            r_raw[gl] = sb("r_raw%d" % gl, [P, PACK, H], BF16)
+            rows = w_rem[gl * KP : (gl + 1) * KP, :].rearrange("(m t r) h -> r m t h", t=PACK, r=RUN)
+            for r in range(RUN):
+                nc.sync.dma_start(out=r_raw[gl][r:P:RUN, :, :], in_=rows[r])
+
+        def group_p(G, g, engine, lo=0, hi=KP):
+            if (G, g) not in p_grp:
+                p_grp[G, g] = sb("p_grp%d%d" % (G, g), [P, KP, PACK], BF16, tag="p_grp", bufs=3)
+            interleave(engine, p_grp[G, g], p_raw[G, g], lo, hi)
+
+        def quant_p(G, g, lo=0, hi=KP):
+            if lo == 0:
+                p_codes[G, g] = sb("p_codes%d%d" % (G, g), [P, KP], U32)
+                p_scales[G, g] = sb("p_scales%d%d" % (G, g), [P, KP], U8)
+            quantize(p_codes[G, g][:, lo:hi], p_scales[G, g][:, lo:hi], p_grp[G, g][:, lo:hi, :])
+
+        def order_z(gl):
+            z_codes[gl] = sb("z_codes%d" % gl, [P, 2, KP], U32)
+            nc.vector.tensor_copy(
+                out=z_codes[gl][:].bitcast(I32).rearrange("p g (t m r) -> p g t m r", t=PACK, r=RUN),
+                in_=z_raw[gl][:].bitcast(I32).rearrange("p g (m t r) -> p g t m r", t=PACK, r=RUN),
+            )
+
+        def order_zs():
+            nc.vector.tensor_copy(
+                out=zs[:].rearrange("p g n -> p (g n)").bitcast(I32).rearrange("p (g t m) -> p g t m", t=PACK, m=P // RUN),
+                in_=zs_raw[:].rearrange("p g n -> p (g n)").bitcast(I32).rearrange("p (g m t) -> p g t m", t=PACK, m=P // RUN),
+            )
+
+        def x_matmul(out, G, gl, t, cols):
+            for g in range(2):
+                nc.tensor.matmul_mx(
+                    out=out,
+                    lhsT=z_codes[gl][:, g, t * P : (t + 1) * P].bitcast(FP8X4),
+                    lhsT_scale=zs[:, g, gl * KP + t * P : gl * KP + (t + 1) * P],
+                    rhs=p_codes[G, g][:, cols].bitcast(FP8X4),
+                    rhs_scale=p_scales[G, g][:, cols],
+                    start=(g == 0),
+                    stop=(g == 1),
+                )
+
+        def new_x(G, gl):
+            x_grp[G, gl] = sb("x_grp%d%d" % (G, gl), [P, KP, PACK], BF16, tag="x_grp", bufs=3)
+
+        def x_vector(G, gl, cc):
+            acc = bank("xv%d%d%d" % (G, gl, cc), [P, PACK, P])
+            for t in range(PACK):
+                x_matmul(acc[:, t, :], G, gl, t, slice(cc * P, (cc + 1) * P))
+            m = P // PACK
+            out = x_grp[G, gl][:].rearrange("p (u m) t -> p u m t", u=PACK)[:, :, cc * m : (cc + 1) * m, :]
+            g4 = gain[:, gl * PACK : (gl + 1) * PACK].unsqueeze(1).unsqueeze(1).to_broadcast([P, PACK, m, PACK])
+            nc.vector.tensor_tensor(out=out, in0=acc[:].rearrange("p t (m u) -> p u m t", u=PACK), in1=g4, op=ALU.mult)
+
+        def x_scalar(G, gl, t):
+            if t == 0:
+                x_slots[G, gl] = sb("x_slots%d%d" % (G, gl), [P, PACK, KP], BF16, tag="x_slots", bufs=2)
+            acc = bank("xs%d%d%d" % (G, gl, t), [P, KP])
+            x_matmul(acc[:], G, gl, t, slice(0, KP))
+            nc.scalar.activation(
+                out=x_slots[G, gl][:, t, :].rearrange("p (u m) -> p u m", u=PACK),
+                in_=acc[:].rearrange("p (m u) -> p u m", u=PACK),
+                func=ACT.Copy,
+                scale=gain[:, gl * PACK + t : gl * PACK + t + 1],
+            )
+
+        def group_x(G, gl):
+            new_x(G, gl)
+            interleave("vector", x_grp[G, gl], x_slots[G, gl], 0, KP)
+
+        def quant_x(G, gl):
+            x_codes[G, gl] = sb("x_codes%d%d" % (G, gl), [P, KP], U32)
+            x_scales[G, gl] = sb("x_scales%d%d" % (G, gl), [P, KP], U8)
+            quantize(x_codes[G, gl][:], x_scales[G, gl][:], x_grp[G, gl][:])
+
+        def turn_a(gl, gj, half):
+            if half == 0:
+                a_grp[gl, gj] = sb("a_grp%d%d" % (gl, gj), [P, KP, PACK], BF16, tag="a_grp", bufs=2)
+            acc = bank("at%d%d%d" % (gl, gj, half), [P, 2, 2, P])
+            words = a_raw[gl, gj][:].bitcast(F32)
+            for u in range(2):
+                for a in range(2):
+                    nc.tensor.transpose(acc[:, u, a, :], words[:, 2 * half + a, u : 2 * P : 2], ident[:])
+            out = a_grp[gl, gj][:].rearrange("p c t -> p (c t)").bitcast(F32)
+            out = out.rearrange("p (t m r u) -> p t m r u", t=PACK, r=RUN, u=2)[:, :, 16 * half : 16 * (half + 1), :, :]
+            in_ = acc[:].rearrange("p u a n -> p u (a n)").rearrange("p u (m t r) -> p t m r u", t=PACK, r=RUN)
+            nc.scalar.copy(out=out, in_=in_)
+
+        def quant_a(gl, gj):
+            a_codes[gl, gj] = sb("a_codes%d%d" % (gl, gj), [P, KP], U32)
+            a_scales[gl, gj] = sb("a_scales%d%d" % (gl, gj), [P, KP], U8)
+            quantize(a_codes[gl, gj][:], a_scales[gl, gj][:], a_grp[gl, gj][:])
+
+        def v_part(gl, hc):
+            if hc == 0:
+                v_grp[gl] = sb("v_grp%d" % gl, [P, H, PACK], BF16)
+            acc = bank("v%d%d" % (gl, hc), [P, PACK, P])
+            for t in range(PACK):
+                for gj in range(2):
+                    nc.tensor.matmul_mx(
+                        out=acc[:, t, :],
+                        lhsT=a_codes[gl, gj][:, t * P : (t + 1) * P].bitcast(FP8X4),
+                        lhsT_scale=a_scales[gl, gj][:, t * P : (t + 1) * P],
+                        rhs=dw[:, gj, 2 * hc * P : 2 * (hc + 1) * P].bitcast(FP4X4),
+                        rhs_scale=ds[:, gj, hc * P : (hc + 1) * P],
+                        start=(gj == 0),
+                        stop=(gj == 1),
+                    )
+            nc.vector.tensor_tensor(
+                out=v_grp[gl][:, hc * P : (hc + 1) * P, :].rearrange("p (c i) t -> p c t i", i=RUN),
+                in0=acc[:].rearrange("p t (c i) -> p c t i", i=RUN),
+                in1=r_raw[gl][:, :, hc * P : (hc + 1) * P].rearrange("p t (c i) -> p c t i", i=RUN),
+                op=ALU.add,
+            )
+
+        def quant_v(gl):
+            v_codes[gl] = sb("v_codes%d" % gl, [P, H], U32)
+            v_scales[gl] = sb("v_scales%d" % gl, [P, H], U8)
+            quantize(v_codes[gl][:], v_scales[gl][:], v_grp[gl][:])
+
+        def make_offset(G, u):
+            k = G * PACK + u
+            offset[G, u] = sb("offset%d%d" % (G, u), [P, H], F32, tag="offset", bufs=12)
+            nc.scalar.activation(
+                out=offset[G, u][:], in_=hb_all[:], func=ACT.Identity,
+                scale=ch[:, 0, k : k + 1], bias=ch[:, 1, k : k + 1],
+            )
+
+        def y_part(G, u):
+            if u == 0:
+                y32[G] = sb("y32_%d" % G, [P, PACK, H], F32)
+            acc = bank("y%d%d" % (G, u), [P, H])
+            for gl in range(2):
+                nc.tensor.matmul_mx(
+                    out=acc[:],
+                    lhsT=x_codes[G, gl][:, u * P : (u + 1) * P].bitcast(FP8X4),
+                    lhsT_scale=x_scales[G, gl][:, u * P : (u + 1) * P],
+                    rhs=v_codes[gl][:].bitcast(FP8X4),
+                    rhs_scale=v_scales[gl][:],
+                    start=(gl == 0),
+                    stop=(gl == 1),
+                )
+            k = G * PACK + u
+            nc.vector.scalar_tensor_tensor(
+                out=y32[G][:, u, :], in0=acc[:], scalar=ch[:, 0, k : k + 1], in1=offset[G, u][:],
+                op0=ALU.mult, op1=ALU.add,
+            )
+
+        def store_y(G, lo, hi):
+            dst = out_0[G * KP : (G + 1) * KP, :].rearrange("(p t) h -> p t h", t=PACK)
+            nc.sync.dma_start(out=dst[:, lo:hi, :], in_=y32[G][:, lo:hi, :])
+
+        def group_y(G, split):
+            y_grp[G] = sb("y_grp%d" % G, [P, H, PACK], BF16, tag="y_grp", bufs=2)
+            if split < H:
+                interleave("scalar", y_grp[G], y32[G], split, H)
+            if split > 0:
+                interleave("vector", y_grp[G], y32[G], 0, split)
+
+        def quant_y(G):
+            y_codes[G] = sb("y_codes%d" % G, [P, H], U32)
+            quantize(y_codes[G][:], y_scales[:, G, :], y_grp[G][:])
+            dst = out_1[G].rearrange("p m t -> p (m t)").bitcast(I32)
+            nc.sync.dma_start(out=dst, in_=y_codes[G][:].bitcast(I32))
+
+        nc.vector.memset(gain_rows[:], 0.0)
+        nc.vector.memset(zs_raw[:].rearrange("p g n -> p (g n)").bitcast(I32), 0)
+        nc.vector.memset(ds[:].rearrange("p g n -> p (g n)").bitcast(I32), 0)
+        load_p(0, 0, 0, 256)
+        load_z(0)
+        load_plane(nc.sync, zs_raw, series_scales)
+        load_p(0, 1, 0, 256)
+        load_p(0, 0, 256, KP)
+        load_p(0, 1, 256, KP)
+        nc.gpsimd.dma_start(out=hb_words[:], in_=h_bias.rearrange("(p t) -> p t", t=PACK))
+        for gl in range(2):
+            nc.gpsimd.dma_start(
+                out=gain_rows[PACK * gl : PACK * (gl + 1), :].rearrange("t (m r) -> t m r", r=RUN),
+                in_=time_gain[gl * KP : (gl + 1) * KP].rearrange("(m t r) -> t m r", t=PACK, r=RUN),
+            )
+        make_identity(nc, ident[:])
+        for i, vec in enumerate((ch_scale, ch_level)):
+            nc.gpsimd.dma_start(
+                out=ch_raw[:, i, 0 : NG * PACK].rearrange("p (g t) -> p g t", t=PACK),
+                in_=vec.rearrange("(g p t) -> p g t", p=P, t=PACK),
+            )
+        nc.scalar.copy(out=ident_bf[:], in_=ident[:])
+        load_a(0, 0)
+        load_a(0, 1)
+        load_z(1)
+        load_p(1, 0)
+        load_a(1, 0)
+        load_a(1, 1)
+        load_d()
+        load_r(0)
+        load_p(1, 1)
+        load_r(1)
+        hb_bank = bank("hb_bank", [P, 2, P])
+        for w in range(2):
+            nc.tensor.transpose(hb_bank[:, w, :], hb_words[:].bitcast(F32)[:, w : w + 1].to_broadcast([P, P]), ident[:])
+        gain_bank = bank("gain_bank", [P, P], BF16)
+        nc.tensor.transpose(gain_bank[:], gain_rows[:], ident_bf[:])
+
+        group_p(0, 0, "scalar", 160, 256)
+        group_p(0, 0, "vector", 0, 160)
+        order_zs()
+        quant_p(0, 0, 0, 256)
+        order_z(0)
+        nc.scalar.copy(
+            out=hb_all[:].bitcast(F32).rearrange("p (n w) -> p n w", w=2), in_=hb_bank[:].rearrange("p w n -> p n w")
+        )
+        group_p(0, 1, "scalar", 160, 256)
+        group_p(0, 1, "vector", 0, 160)
+        group_p(0, 0, "scalar", 256, KP)
+        nc.scalar.copy(out=gain[:], in_=gain_bank[:, 0 : 2 * PACK])
+        nc.scalar.copy(out=ch[:], in_=ch_raw[:, :, 0 : NG * PACK])
+        group_p(0, 1, "vector", 256, KP)
+        quant_p(0, 1, 0, 256)
+        load_p(2, 0)
+        load_p(2, 1)
+        quant_p(0, 0, 256, KP)
+        new_x(0, 0)
+        x_vector(0, 0, 0)
+        quant_p(0, 1, 256, KP)
+        for k in range(0, 6):
+            make_offset(k // 4, k % 4)
+        x_vector(0, 0, 1)
+        x_vector(0, 0, 2)
+        x_vector(0, 0, 3)
+        order_z(1)
+        for gj in range(2):
+            for half in range(2):
+                turn_a(0, gj, half)
+        group_p(1, 0, "scalar")
+        quant_x(0, 0)
+        quant_a(0, 0)
+        new_x(0, 1)
+        x_vector(0, 1, 0)
+        quant_a(0, 1)
+        x_vector(0, 1, 1)
+        x_vector(0, 1, 2)
+        quant_p(1, 0)
+        x_vector(0, 1, 3)
+        for gj in range(2):
+            for half in range(2):
+                turn_a(1, gj, half)
+        for k in range(6, 8):
+            make_offset(k // 4, k % 4)
+        group_p(1, 1, "scalar")
+        group_p(2, 0, "scalar")
+        quant_a(1, 0)
+        quant_x(0, 1)
+        v_part(0, 0)
+        quant_a(1, 1)
+        v_part(0, 1)
+        v_part(0, 2)
+        v_part(0, 3)
+        v_part(1, 0)
+        quant_p(1, 1)
+        v_part(1, 1)
+        quant_v(0)
+        v_part(1, 2)
+        v_part(1, 3)
+        for t in range(4):
+            x_scalar(1, 0, t)
+        quant_p(2, 0)
+        quant_v(1)
+        group_p(2, 1, "scalar")
+        for t in range(2):
+            x_scalar(1, 1, t)
+        y_part(0, 0)
+        group_x(1, 0)
+        y_part(0, 1)
+        quant_p(2, 1)
+        y_part(0, 2)
+        quant_x(1, 0)
+        y_part(0, 3)
+        store_y(0, 0, 4)
+        for t in range(2, 4):
+            x_scalar(1, 1, t)
+        for t in range(4):
+            x_scalar(2, 0, t)
+        group_x(1, 1)
+        for t in range(4):
+            x_scalar(2, 1, t)
+        for k in range(8, 8):
+            make_offset(k // 4, k % 4)
+        group_y(0, 0)
+        for k in range(8, 12):
+            make_offset(k // 4, k % 4)
+        quant_x(1, 1)
+        group_x(2, 0)
+        y_part(1, 0)
+        store_y(1, 0, 1)
+        quant_x(2, 0)
+        group_x(2, 1)
+        y_part(1, 1)
+        store_y(1, 1, 2)
+        quant_x(2, 1)
+        for u in range(2, 4):
+            y_part(1, u)
+            store_y(1, u, u + 1)
+        quant_y(0)
+        group_y(1, 0)
+        for u in range(4):
+            y_part(2, u)
+            store_y(2, u, u + 1)
+        group_y(2, 352)
+        quant_y(1)
+        quant_y(2)
+        for q in range(4):
+            queue = nc.scalar if q % 2 == 0 else nc.sync
+            queue.dma_start(
+                out=out_2[:, 4 * q : 4 * q + 4, :].rearrange("g r m -> r g m").bitcast(I32),
+                in_=y_scales[32 * q : 32 * q + 4, :, :].bitcast(I32),
+            )

@@ -56,8 +56,9 @@ def tile_merged_dlinear_style_forecast_k4_kernel(
         zs = sb("zs", [P, 2, L], U8)
         ds = sb("ds", [P, 2, H], U8)
         dw = sb("dw", [P, 2, 2 * H], U8)
-        gain_rows = sb("gain_rows", [P, P], BF16)
-        gain = sb("gain", [P, 2 * PACK], F32)
+        gain_raw = sb("gain_raw", [2, KP], BF16)
+        gain_rows = sb("gain_rows", [P, KP], BF16)
+        gain = sb("gain", [P, 2, PACK], F32)
         hb_words = sb("hb_words", [P, PACK], BF16)
         hb_all = sb("hb_all", [P, H], BF16)
         ch_raw = sb("ch_raw", [P, 2, 16], BF16)
@@ -72,10 +73,12 @@ def tile_merged_dlinear_style_forecast_k4_kernel(
         offset, y32, y_grp, y_codes = {}, {}, {}, {}
 
         def load_p(G, g, lo=0, hi=KP):
-            if lo == 0:
-                p_raw[G, g] = sb("p_raw%d%d" % (G, g), [P, PACK, KP], BF16, tag="p_raw", bufs=4)
+            if hi - lo == KP:
+                p_raw[G, g, lo] = sb("p_raw%d%d" % (G, g), [P, PACK, KP], BF16, tag="p_raw", bufs=3)
+            else:
+                p_raw[G, g, lo] = sb("p_half%d%d" % (g, lo), [P, PACK, hi - lo], BF16)
             src = mix[g * KP : (g + 1) * KP, G * KP + lo : G * KP + hi].rearrange("(p j) c -> p j c", j=PACK)
-            nc.sync.dma_start(out=p_raw[G, g][:, :, lo:hi], in_=src)
+            nc.sync.dma_start(out=p_raw[G, g, lo][:], in_=src)
 
         def load_z(gl):
             z_raw[gl] = sb("z_raw%d" % gl, [P, 2, KP], U32)
@@ -102,10 +105,16 @@ def tile_merged_dlinear_style_forecast_k4_kernel(
             for r in range(RUN):
                 nc.sync.dma_start(out=r_raw[gl][r:P:RUN, :, :], in_=rows[r])
 
-        def group_p(G, g, engine, lo=0, hi=KP):
+        def group_p(G, g, engine, u0=0, u1=PACK, base=0, width=KP):
             if (G, g) not in p_grp:
                 p_grp[G, g] = sb("p_grp%d%d" % (G, g), [P, KP, PACK], BF16, tag="p_grp", bufs=3)
-            interleave(engine, p_grp[G, g], p_raw[G, g], lo, hi)
+            out = p_grp[G, g][:, base : base + width, :].rearrange("p (u n i) j -> p n u i j", u=PACK, i=2)
+            out = out[:, :, u0:u1]
+            in_ = p_raw[G, g, base][:].rearrange("p j (n i u) -> p n u i j", u=PACK, i=2)[:, :, u0:u1]
+            if engine == "vector":
+                nc.vector.tensor_copy(out=out, in_=in_)
+            else:
+                nc.scalar.copy(out=out, in_=in_)
 
         def quant_p(G, g, lo=0, hi=KP):
             if lo == 0:
@@ -145,10 +154,10 @@ def tile_merged_dlinear_style_forecast_k4_kernel(
             acc = bank("xv%d%d%d" % (G, gl, cc), [P, PACK, P])
             for t in range(PACK):
                 x_matmul(acc[:, t, :], G, gl, t, slice(cc * P, (cc + 1) * P))
-            m = P // PACK
-            out = x_grp[G, gl][:].rearrange("p (u m) t -> p u m t", u=PACK)[:, :, cc * m : (cc + 1) * m, :]
-            g4 = gain[:, gl * PACK : (gl + 1) * PACK].unsqueeze(1).unsqueeze(1).to_broadcast([P, PACK, m, PACK])
-            nc.vector.tensor_tensor(out=out, in0=acc[:].rearrange("p t (m u) -> p u m t", u=PACK), in1=g4, op=ALU.mult)
+            half, u0 = cc // 2, 2 * (cc % 2)
+            out = x_grp[G, gl][:].rearrange("p (u h m) t -> p u h m t", u=PACK, h=2)[:, u0 : u0 + 2, half]
+            g4 = gain[:, gl, :].unsqueeze(1).unsqueeze(1).to_broadcast([P, 2, P // 2, PACK])
+            nc.vector.tensor_tensor(out=out, in0=acc[:].rearrange("p t (u m) -> p u m t", u=2), in1=g4, op=ALU.mult)
 
         def x_scalar(G, gl, t):
             if t == 0:
@@ -156,10 +165,7 @@ def tile_merged_dlinear_style_forecast_k4_kernel(
             acc = bank("xs%d%d%d" % (G, gl, t), [P, KP])
             x_matmul(acc[:], G, gl, t, slice(0, KP))
             nc.scalar.activation(
-                out=x_slots[G, gl][:, t, :].rearrange("p (u m) -> p u m", u=PACK),
-                in_=acc[:].rearrange("p (m u) -> p u m", u=PACK),
-                func=ACT.Copy,
-                scale=gain[:, gl * PACK + t : gl * PACK + t + 1],
+                out=x_slots[G, gl][:, t, :], in_=acc[:], func=ACT.Copy, scale=gain[:, gl, t : t + 1],
             )
 
         def group_x(G, gl):
@@ -216,13 +222,19 @@ def tile_merged_dlinear_style_forecast_k4_kernel(
             v_scales[gl] = sb("v_scales%d" % gl, [P, H], U8)
             quantize(v_codes[gl][:], v_scales[gl][:], v_grp[gl][:])
 
-        def make_offset(G, u):
-            k = G * PACK + u
-            offset[G, u] = sb("offset%d%d" % (G, u), [P, H], F32, tag="offset", bufs=12)
-            nc.scalar.activation(
-                out=offset[G, u][:], in_=hb_all[:], func=ACT.Identity,
-                scale=ch[:, 0, k : k + 1], bias=ch[:, 1, k : k + 1],
-            )
+        def make_offset(k, engine):
+            G, u = divmod(k, PACK)
+            offset[G, u] = sb("offset%d%d" % (G, u), [P, H], F32)
+            if engine == "scalar":
+                nc.scalar.activation(
+                    out=offset[G, u][:], in_=hb_all[:], func=ACT.Identity,
+                    scale=ch[:, 0, k : k + 1], bias=ch[:, 1, k : k + 1],
+                )
+            else:
+                nc.gpsimd.tensor_scalar(
+                    out=offset[G, u][:], in0=hb_all[:], scalar1=ch[:, 0, k : k + 1], scalar2=ch[:, 1, k : k + 1],
+                    op0=ALU.mult, op1=ALU.add,
+                )
 
         def y_part(G, u):
             if u == 0:
@@ -261,28 +273,24 @@ def tile_merged_dlinear_style_forecast_k4_kernel(
             dst = out_1[G].rearrange("p m t -> p (m t)").bitcast(I32)
             nc.sync.dma_start(out=dst, in_=y_codes[G][:].bitcast(I32))
 
-        nc.vector.memset(gain_rows[:], 0.0)
         nc.vector.memset(zs_raw[:].rearrange("p g n -> p (g n)").bitcast(I32), 0)
+        nc.vector.memset(gain_rows[:], 0.0)
         nc.vector.memset(ds[:].rearrange("p g n -> p (g n)").bitcast(I32), 0)
+        make_identity(nc, ident[:])
+        nc.gpsimd.dma_start(out=hb_words[:], in_=h_bias.rearrange("(p t) -> p t", t=PACK))
+        nc.scalar.copy(out=ident_bf[:], in_=ident[:])
         load_p(0, 0, 0, 256)
-        load_z(0)
         load_plane(nc.sync, zs_raw, series_scales)
+        nc.sync.dma_start(out=gain_raw[:], in_=time_gain.rearrange("(g l) -> g l", g=2))
+        load_z(0)
         load_p(0, 1, 0, 256)
         load_p(0, 0, 256, KP)
         load_p(0, 1, 256, KP)
-        nc.gpsimd.dma_start(out=hb_words[:], in_=h_bias.rearrange("(p t) -> p t", t=PACK))
-        for gl in range(2):
-            nc.gpsimd.dma_start(
-                out=gain_rows[PACK * gl : PACK * (gl + 1), :].rearrange("t (m r) -> t m r", r=RUN),
-                in_=time_gain[gl * KP : (gl + 1) * KP].rearrange("(m t r) -> t m r", t=PACK, r=RUN),
-            )
-        make_identity(nc, ident[:])
         for i, vec in enumerate((ch_scale, ch_level)):
-            nc.gpsimd.dma_start(
+            nc.sync.dma_start(
                 out=ch_raw[:, i, 0 : NG * PACK].rearrange("p (g t) -> p g t", t=PACK),
                 in_=vec.rearrange("(g p t) -> p g t", p=P, t=PACK),
             )
-        nc.scalar.copy(out=ident_bf[:], in_=ident[:])
         load_a(0, 0)
         load_a(0, 1)
         load_z(1)
@@ -293,35 +301,41 @@ def tile_merged_dlinear_style_forecast_k4_kernel(
         load_r(0)
         load_p(1, 1)
         load_r(1)
+        group_p(0, 0, "scalar", 2, PACK, 0, 256)
+        group_p(0, 0, "vector", 0, 2, 0, 256)
+        nc.scalar.copy(
+            out=gain_rows[0:2, :].rearrange("g (t m r) -> g t m r", t=PACK, r=RUN),
+            in_=gain_raw[:].rearrange("g (m t r) -> g t m r", t=PACK, r=RUN),
+        )
         hb_bank = bank("hb_bank", [P, 2, P])
         for w in range(2):
             nc.tensor.transpose(hb_bank[:, w, :], hb_words[:].bitcast(F32)[:, w : w + 1].to_broadcast([P, P]), ident[:])
-        gain_bank = bank("gain_bank", [P, P], BF16)
-        nc.tensor.transpose(gain_bank[:], gain_rows[:], ident_bf[:])
+        gain_bank = bank("gain_bank", [P, PACK, P], BF16)
+        for t in range(PACK):
+            nc.tensor.transpose(gain_bank[:, t, :], gain_rows[:, t * P : (t + 1) * P], ident_bf[:])
 
-        group_p(0, 0, "scalar", 160, 256)
-        group_p(0, 0, "vector", 0, 160)
-        order_zs()
-        quant_p(0, 0, 0, 256)
-        order_z(0)
         nc.scalar.copy(
             out=hb_all[:].bitcast(F32).rearrange("p (n w) -> p n w", w=2), in_=hb_bank[:].rearrange("p w n -> p n w")
         )
-        group_p(0, 1, "scalar", 160, 256)
-        group_p(0, 1, "vector", 0, 160)
-        group_p(0, 0, "scalar", 256, KP)
-        nc.scalar.copy(out=gain[:], in_=gain_bank[:, 0 : 2 * PACK])
-        nc.scalar.copy(out=ch[:], in_=ch_raw[:, :, 0 : NG * PACK])
-        group_p(0, 1, "vector", 256, KP)
+        order_zs()
+        quant_p(0, 0, 0, 256)
+        order_z(0)
+        group_p(0, 1, "scalar", 3, PACK, 0, 256)
+        group_p(0, 1, "vector", 0, 3, 0, 256)
+        group_p(0, 0, "scalar", 0, PACK, 256, 256)
         quant_p(0, 1, 0, 256)
+        nc.scalar.copy(out=gain[:], in_=gain_bank[:, :, 0:2].rearrange("p t g -> p g t"))
+        group_p(0, 1, "vector", 0, 4, 256, 256)
+        nc.scalar.copy(out=ch[:], in_=ch_raw[:, :, 0 : NG * PACK])
         load_p(2, 0)
-        load_p(2, 1)
         quant_p(0, 0, 256, KP)
         new_x(0, 0)
         x_vector(0, 0, 0)
         quant_p(0, 1, 256, KP)
-        for k in range(0, 6):
-            make_offset(k // 4, k % 4)
+        for k in range(5):
+            make_offset(k, "scalar")
+        for k in range(5, 9):
+            make_offset(k, "gpsimd")
         x_vector(0, 0, 1)
         x_vector(0, 0, 2)
         x_vector(0, 0, 3)
@@ -330,6 +344,7 @@ def tile_merged_dlinear_style_forecast_k4_kernel(
             for half in range(2):
                 turn_a(0, gj, half)
         group_p(1, 0, "scalar")
+        load_p(2, 1)
         quant_x(0, 0)
         quant_a(0, 0)
         new_x(0, 1)
@@ -342,8 +357,6 @@ def tile_merged_dlinear_style_forecast_k4_kernel(
         for gj in range(2):
             for half in range(2):
                 turn_a(1, gj, half)
-        for k in range(6, 8):
-            make_offset(k // 4, k % 4)
         group_p(1, 1, "scalar")
         group_p(2, 0, "scalar")
         quant_a(1, 0)
@@ -381,11 +394,9 @@ def tile_merged_dlinear_style_forecast_k4_kernel(
         group_x(1, 1)
         for t in range(4):
             x_scalar(2, 1, t)
-        for k in range(8, 8):
-            make_offset(k // 4, k % 4)
         group_y(0, 0)
-        for k in range(8, 12):
-            make_offset(k // 4, k % 4)
+        for k in range(9, 12):
+            make_offset(k, "scalar")
         quant_x(1, 1)
         group_x(2, 0)
         y_part(1, 0)

@@ -52,8 +52,8 @@ def tile_merged_dlinear_style_forecast_k4_kernel(
 
         ident = sb("ident", [P, P], F32)
         ident_bf = sb("ident_bf", [P, P], BF16)
-        zs_raw = sb("zs_raw", [P, 2, L], U8)
-        zs = sb("zs", [P, 2, L], U8)
+        zs_raw = sb("zs_raw", [P, L], U8)
+        zs = sb("zs", [P, L], U8)
         ds = sb("ds", [P, 2, H], U8)
         dw = sb("dw", [P, 2, 2 * H], U8)
         gain_raw = sb("gain_raw", [2, KP], BF16)
@@ -73,27 +73,34 @@ def tile_merged_dlinear_style_forecast_k4_kernel(
         offset, y32, y_grp, y_codes = {}, {}, {}, {}
 
         def load_p(G, g, lo=0, hi=KP):
-            if hi - lo == KP:
-                p_raw[G, g, lo] = sb("p_raw%d%d" % (G, g), [P, PACK, KP], BF16, tag="p_raw", bufs=3)
-            else:
-                p_raw[G, g, lo] = sb("p_half%d%d" % (g, lo), [P, PACK, hi - lo], BF16)
+            raw = sb("p_raw%d%d_%d" % (G, g, lo), [P, PACK, hi - lo], BF16)
             src = mix[g * KP : (g + 1) * KP, G * KP + lo : G * KP + hi].rearrange("(p j) c -> p j c", j=PACK)
-            nc.sync.dma_start(out=p_raw[G, g, lo][:], in_=src)
+            nc.sync.dma_start(out=raw[:], in_=src)
+            if hi - lo <= KP:
+                p_raw[G, g, lo] = raw[:]
+            else:
+                for i in range((hi - lo) // KP):
+                    p_raw[G + i, g, 0] = raw[:, :, i * KP : (i + 1) * KP]
 
-        def load_z(gl):
-            z_raw[gl] = sb("z_raw%d" % gl, [P, 2, KP], U32)
-            src = series_words.rearrange("g p n t -> p g (n t)")[:, :, gl * KP * 4 : (gl + 1) * KP * 4].bitcast(I32)
-            nc.sync.dma_start(out=z_raw[gl][:].bitcast(I32), in_=src)
+        def load_z(gl, g0=0, g1=2):
+            z_raw[gl, g0] = sb("z_raw%d%d" % (gl, g0), [P, g1 - g0, KP], U32)
+            src = series_words.rearrange("g p n t -> p g (n t)")[:, g0:g1, gl * KP * 4 : (gl + 1) * KP * 4].bitcast(I32)
+            nc.sync.dma_start(out=z_raw[gl, g0][:].bitcast(I32), in_=src)
 
         def load_plane(queue, plane, rows):
             for q in range(4):
                 src = rows[:, 4 * q : 4 * q + 4, :].rearrange("g r n -> r g n").bitcast(I32)
                 queue.dma_start(out=plane[32 * q : 32 * q + 4, :, :].bitcast(I32), in_=src)
 
-        def load_a(gl, gj):
-            a_raw[gl, gj] = sb("a_raw%d%d" % (gl, gj), [P, PACK, KP], BF16)
-            src = avg[gl * KP : (gl + 1) * KP, gj * KP : (gj + 1) * KP].rearrange("(a p) j -> p a j", p=P)
-            nc.sync.dma_start(out=a_raw[gl, gj][:], in_=src)
+        def load_zs():
+            for q in range(4):
+                src = series_scales[:, 4 * q : 4 * q + 4, :].bitcast(I32)
+                nc.sync.dma_start(out=zs_raw[32 * q : 32 * q + 8, :].bitcast(I32), in_=src)
+
+        def load_a(gl, half):
+            a_raw[gl, half] = sb("a_raw%d%d" % (gl, half), [P, 2, L], BF16)
+            src = avg[gl * KP : (gl + 1) * KP, :].rearrange("(p a) j -> p a j", a=RUN)
+            nc.sync.dma_start(out=a_raw[gl, half][:], in_=src[:, 2 * half : 2 * half + 2, :])
 
         def load_d():
             load_plane(nc.sync, ds, diff_scales)
@@ -107,10 +114,10 @@ def tile_merged_dlinear_style_forecast_k4_kernel(
 
         def group_p(G, g, engine, u0=0, u1=PACK, base=0, width=KP):
             if (G, g) not in p_grp:
-                p_grp[G, g] = sb("p_grp%d%d" % (G, g), [P, KP, PACK], BF16, tag="p_grp", bufs=3)
+                p_grp[G, g] = sb("p_grp%d%d" % (G, g), [P, KP, PACK], BF16, tag="grp", bufs=10)
             out = p_grp[G, g][:, base : base + width, :].rearrange("p (u n i) j -> p n u i j", u=PACK, i=2)
             out = out[:, :, u0:u1]
-            in_ = p_raw[G, g, base][:].rearrange("p j (n i u) -> p n u i j", u=PACK, i=2)[:, :, u0:u1]
+            in_ = p_raw[G, g, base].rearrange("p j (n i u) -> p n u i j", u=PACK, i=2)[:, :, u0:u1]
             if engine == "vector":
                 nc.vector.tensor_copy(out=out, in_=in_)
             else:
@@ -122,25 +129,27 @@ def tile_merged_dlinear_style_forecast_k4_kernel(
                 p_scales[G, g] = sb("p_scales%d%d" % (G, g), [P, KP], U8)
             quantize(p_codes[G, g][:, lo:hi], p_scales[G, g][:, lo:hi], p_grp[G, g][:, lo:hi, :])
 
-        def order_z(gl):
-            z_codes[gl] = sb("z_codes%d" % gl, [P, 2, KP], U32)
+        def order_z(gl, g0=0, g1=2):
+            codes = sb("z_codes%d%d" % (gl, g0), [P, g1 - g0, KP], U32)
             nc.vector.tensor_copy(
-                out=z_codes[gl][:].bitcast(I32).rearrange("p g (t m r) -> p g t m r", t=PACK, r=RUN),
-                in_=z_raw[gl][:].bitcast(I32).rearrange("p g (m t r) -> p g t m r", t=PACK, r=RUN),
+                out=codes[:].bitcast(I32).rearrange("p g (t m r) -> p g t m r", t=PACK, r=RUN),
+                in_=z_raw[gl, g0][:].bitcast(I32).rearrange("p g (m t r) -> p g t m r", t=PACK, r=RUN),
             )
+            for g in range(g0, g1):
+                z_codes[gl, g] = codes[:, g - g0, :]
 
         def order_zs():
             nc.vector.tensor_copy(
-                out=zs[:].rearrange("p g n -> p (g n)").bitcast(I32).rearrange("p (g t m) -> p g t m", t=PACK, m=P // RUN),
-                in_=zs_raw[:].rearrange("p g n -> p (g n)").bitcast(I32).rearrange("p (g m t) -> p g t m", t=PACK, m=P // RUN),
+                out=zs[:].bitcast(I32).rearrange("p (g t m) -> p g t m", t=PACK, m=P // RUN),
+                in_=zs_raw[:].bitcast(I32).rearrange("p (g m t) -> p g t m", t=PACK, m=P // RUN),
             )
 
-        def x_matmul(out, G, gl, t, cols):
-            for g in range(2):
+        def x_matmul(out, G, gl, t, cols, passes=(0, 1)):
+            for g in passes:
                 nc.tensor.matmul_mx(
                     out=out,
-                    lhsT=z_codes[gl][:, g, t * P : (t + 1) * P].bitcast(FP8X4),
-                    lhsT_scale=zs[:, g, gl * KP + t * P : gl * KP + (t + 1) * P],
+                    lhsT=z_codes[gl, g][:, t * P : (t + 1) * P].bitcast(FP8X4),
+                    lhsT_scale=zs[4 * g : P, gl * KP + t * P : gl * KP + (t + 1) * P],
                     rhs=p_codes[G, g][:, cols].bitcast(FP8X4),
                     rhs_scale=p_scales[G, g][:, cols],
                     start=(g == 0),
@@ -148,22 +157,31 @@ def tile_merged_dlinear_style_forecast_k4_kernel(
                 )
 
         def new_x(G, gl):
-            x_grp[G, gl] = sb("x_grp%d%d" % (G, gl), [P, KP, PACK], BF16, tag="x_grp", bufs=3)
+            x_grp[G, gl] = sb("x_grp%d%d" % (G, gl), [P, KP, PACK], BF16, tag="grp", bufs=10)
 
         def x_vector(G, gl, cc):
             acc = bank("xv%d%d%d" % (G, gl, cc), [P, PACK, P])
             for t in range(PACK):
                 x_matmul(acc[:, t, :], G, gl, t, slice(cc * P, (cc + 1) * P))
-            half, u0 = cc // 2, 2 * (cc % 2)
-            out = x_grp[G, gl][:].rearrange("p (u h m) t -> p u h m t", u=PACK, h=2)[:, u0 : u0 + 2, half]
-            g4 = gain[:, gl, :].unsqueeze(1).unsqueeze(1).to_broadcast([P, 2, P // 2, PACK])
-            nc.vector.tensor_tensor(out=out, in0=acc[:].rearrange("p t (u m) -> p u m t", u=2), in1=g4, op=ALU.mult)
+            out = x_grp[G, gl][:, cc * P : (cc + 1) * P, :]
+            g4 = gain[:, gl, :].unsqueeze(1).to_broadcast([P, P, PACK])
+            nc.vector.tensor_tensor(out=out, in0=acc[:].rearrange("p t c -> p c t"), in1=g4, op=ALU.mult)
+
+        opened = {}
+
+        def x_open(G, gl, t):
+            opened[G, gl, t] = bank("xs%d%d%d" % (G, gl, t), [P, KP])
+            x_matmul(opened[G, gl, t][:], G, gl, t, slice(0, KP), (0,))
 
         def x_scalar(G, gl, t):
             if t == 0:
                 x_slots[G, gl] = sb("x_slots%d%d" % (G, gl), [P, PACK, KP], BF16, tag="x_slots", bufs=2)
-            acc = bank("xs%d%d%d" % (G, gl, t), [P, KP])
-            x_matmul(acc[:], G, gl, t, slice(0, KP))
+            if (G, gl, t) in opened:
+                acc = opened[G, gl, t]
+                x_matmul(acc[:], G, gl, t, slice(0, KP), (1,))
+            else:
+                acc = bank("xs%d%d%d" % (G, gl, t), [P, KP])
+                x_matmul(acc[:], G, gl, t, slice(0, KP))
             nc.scalar.activation(
                 out=x_slots[G, gl][:, t, :], in_=acc[:], func=ACT.Copy, scale=gain[:, gl, t : t + 1],
             )
@@ -179,15 +197,15 @@ def tile_merged_dlinear_style_forecast_k4_kernel(
 
         def turn_a(gl, gj, half):
             if half == 0:
-                a_grp[gl, gj] = sb("a_grp%d%d" % (gl, gj), [P, KP, PACK], BF16, tag="a_grp", bufs=2)
+                a_grp[gl, gj] = sb("a_grp%d%d" % (gl, gj), [P, KP, PACK], BF16, tag="grp", bufs=10)
             acc = bank("at%d%d%d" % (gl, gj, half), [P, 2, 2, P])
-            words = a_raw[gl, gj][:].bitcast(F32)
+            words = a_raw[gl, half][:].bitcast(F32)
             for u in range(2):
                 for a in range(2):
-                    nc.tensor.transpose(acc[:, u, a, :], words[:, 2 * half + a, u : 2 * P : 2], ident[:])
+                    nc.tensor.transpose(acc[:, u, a, :], words[:, a, 2 * P * gj + u : 2 * P * (gj + 1) : 2], ident[:])
             out = a_grp[gl, gj][:].rearrange("p c t -> p (c t)").bitcast(F32)
-            out = out.rearrange("p (t m r u) -> p t m r u", t=PACK, r=RUN, u=2)[:, :, 16 * half : 16 * (half + 1), :, :]
-            in_ = acc[:].rearrange("p u a n -> p u (a n)").rearrange("p u (m t r) -> p t m r u", t=PACK, r=RUN)
+            out = out.rearrange("p (t m r u) -> p m t r u", t=PACK, r=RUN, u=2)[:, :, :, 2 * half : 2 * half + 2, :]
+            in_ = acc[:].rearrange("p u r (m t) -> p m t r u", t=PACK)
             nc.scalar.copy(out=out, in_=in_)
 
         def quant_a(gl, gj):
@@ -197,7 +215,7 @@ def tile_merged_dlinear_style_forecast_k4_kernel(
 
         def v_part(gl, hc):
             if hc == 0:
-                v_grp[gl] = sb("v_grp%d" % gl, [P, H, PACK], BF16)
+                v_grp[gl] = sb("v_grp%d" % gl, [P, H, PACK], BF16, tag="grp", bufs=10)
             acc = bank("v%d%d" % (gl, hc), [P, PACK, P])
             for t in range(PACK):
                 for gj in range(2):
@@ -231,7 +249,7 @@ def tile_merged_dlinear_style_forecast_k4_kernel(
                     scale=ch[:, 0, k : k + 1], bias=ch[:, 1, k : k + 1],
                 )
             else:
-                nc.gpsimd.tensor_scalar(
+                (nc.vector if engine == "vector" else nc.gpsimd).tensor_scalar(
                     out=offset[G, u][:], in0=hb_all[:], scalar1=ch[:, 0, k : k + 1], scalar2=ch[:, 1, k : k + 1],
                     op0=ALU.mult, op1=ALU.add,
                 )
@@ -261,7 +279,7 @@ def tile_merged_dlinear_style_forecast_k4_kernel(
             nc.sync.dma_start(out=dst[:, lo:hi, :], in_=y32[G][:, lo:hi, :])
 
         def group_y(G, split):
-            y_grp[G] = sb("y_grp%d" % G, [P, H, PACK], BF16, tag="y_grp", bufs=2)
+            y_grp[G] = sb("y_grp%d" % G, [P, H, PACK], BF16, tag="grp", bufs=10)
             if split < H:
                 interleave("scalar", y_grp[G], y32[G], split, H)
             if split > 0:
@@ -273,27 +291,47 @@ def tile_merged_dlinear_style_forecast_k4_kernel(
             dst = out_1[G].rearrange("p m t -> p (m t)").bitcast(I32)
             nc.sync.dma_start(out=dst, in_=y_codes[G][:].bitcast(I32))
 
-        nc.vector.memset(zs_raw[:].rearrange("p g n -> p (g n)").bitcast(I32), 0)
+        def consts_gain():
+            nc.scalar.copy(
+                out=gain_rows[0:2, :].rearrange("g (t m r) -> g t m r", t=PACK, r=RUN),
+                in_=gain_raw[:].rearrange("g (m t r) -> g t m r", t=PACK, r=RUN),
+            )
+            gain_bank = bank("gain_bank", [P, PACK, P], BF16)
+            for t in range(PACK):
+                nc.tensor.transpose(gain_bank[:, t, :], gain_rows[:, t * P : (t + 1) * P], ident_bf[:])
+            return gain_bank
+
+        def consts_hb():
+            hb_bank = bank("hb_bank", [P, 2, P])
+            for w in range(2):
+                nc.tensor.transpose(hb_bank[:, w, :], hb_words[:].bitcast(F32)[:, w : w + 1].to_broadcast([P, P]), ident[:])
+            nc.scalar.copy(
+                out=hb_all[:].bitcast(F32).rearrange("p (n w) -> p n w", w=2), in_=hb_bank[:].rearrange("p w n -> p n w")
+            )
+
+        def load_ch():
+            for i, vec in enumerate((ch_scale, ch_level)):
+                nc.sync.dma_start(
+                    out=ch_raw[:, i, 0 : NG * PACK].rearrange("p (g t) -> p g t", t=PACK),
+                    in_=vec.rearrange("(g p t) -> p g t", p=P, t=PACK),
+                )
+
+        nc.vector.memset(zs_raw[:].bitcast(I32), 0)
         nc.vector.memset(gain_rows[:], 0.0)
         nc.vector.memset(ds[:].rearrange("p g n -> p (g n)").bitcast(I32), 0)
         make_identity(nc, ident[:])
         nc.gpsimd.dma_start(out=hb_words[:], in_=h_bias.rearrange("(p t) -> p t", t=PACK))
         nc.scalar.copy(out=ident_bf[:], in_=ident[:])
-        load_p(0, 0, 0, 256)
-        load_plane(nc.sync, zs_raw, series_scales)
+        load_p(0, 0)
+        load_zs()
         nc.sync.dma_start(out=gain_raw[:], in_=time_gain.rearrange("(g l) -> g l", g=2))
-        load_z(0)
-        load_p(0, 1, 0, 256)
-        load_p(0, 0, 256, KP)
-        load_p(0, 1, 256, KP)
-        for i, vec in enumerate((ch_scale, ch_level)):
-            nc.sync.dma_start(
-                out=ch_raw[:, i, 0 : NG * PACK].rearrange("p (g t) -> p g t", t=PACK),
-                in_=vec.rearrange("(g p t) -> p g t", p=P, t=PACK),
-            )
+        load_z(0, 0, 1)
+        load_p(0, 1)
+        load_z(0, 1, 2)
+        load_ch()
         load_a(0, 0)
-        load_a(0, 1)
         load_z(1)
+        load_a(0, 1)
         load_p(1, 0)
         load_a(1, 0)
         load_a(1, 1)
@@ -301,69 +339,65 @@ def tile_merged_dlinear_style_forecast_k4_kernel(
         load_r(0)
         load_p(1, 1)
         load_r(1)
-        group_p(0, 0, "scalar", 2, PACK, 0, 256)
-        group_p(0, 0, "vector", 0, 2, 0, 256)
-        nc.scalar.copy(
-            out=gain_rows[0:2, :].rearrange("g (t m r) -> g t m r", t=PACK, r=RUN),
-            in_=gain_raw[:].rearrange("g (m t r) -> g t m r", t=PACK, r=RUN),
-        )
-        hb_bank = bank("hb_bank", [P, 2, P])
-        for w in range(2):
-            nc.tensor.transpose(hb_bank[:, w, :], hb_words[:].bitcast(F32)[:, w : w + 1].to_broadcast([P, P]), ident[:])
-        gain_bank = bank("gain_bank", [P, PACK, P], BF16)
-        for t in range(PACK):
-            nc.tensor.transpose(gain_bank[:, t, :], gain_rows[:, t * P : (t + 1) * P], ident_bf[:])
-
-        nc.scalar.copy(
-            out=hb_all[:].bitcast(F32).rearrange("p (n w) -> p n w", w=2), in_=hb_bank[:].rearrange("p w n -> p n w")
-        )
-        order_zs()
-        quant_p(0, 0, 0, 256)
-        order_z(0)
-        group_p(0, 1, "scalar", 3, PACK, 0, 256)
-        group_p(0, 1, "vector", 0, 3, 0, 256)
-        group_p(0, 0, "scalar", 0, PACK, 256, 256)
-        quant_p(0, 1, 0, 256)
-        nc.scalar.copy(out=gain[:], in_=gain_bank[:, :, 0:2].rearrange("p t g -> p g t"))
-        group_p(0, 1, "vector", 0, 4, 256, 256)
-        nc.scalar.copy(out=ch[:], in_=ch_raw[:, :, 0 : NG * PACK])
         load_p(2, 0)
-        quant_p(0, 0, 256, KP)
-        new_x(0, 0)
-        x_vector(0, 0, 0)
-        quant_p(0, 1, 256, KP)
-        for k in range(5):
+        load_p(2, 1)
+        order_zs()
+        gain_bank = consts_gain()
+        group_p(0, 0, "scalar", 3, PACK)
+        group_p(0, 0, "vector", 0, 3)
+        consts_hb()
+        order_z(0, 0, 1)
+        quant_p(0, 0)
+        nc.scalar.copy(out=gain[:], in_=gain_bank[:, :, 0:2].rearrange("p t g -> p g t"))
+        for t in range(4):
+            x_open(0, 0, t)
+        group_p(0, 1, "scalar", 3, PACK)
+        group_p(0, 1, "vector", 0, 3)
+        nc.scalar.copy(out=ch[:], in_=ch_raw[:, :, 0 : NG * PACK])
+        order_z(0, 1, 2)
+        quant_p(0, 1)
+        for k in range(0, 2):
             make_offset(k, "scalar")
-        for k in range(5, 9):
-            make_offset(k, "gpsimd")
-        x_vector(0, 0, 1)
-        x_vector(0, 0, 2)
-        x_vector(0, 0, 3)
+        for t in range(4):
+            x_scalar(0, 0, t)
+        for k in range(2, 6):
+            make_offset(k, "vector")
         order_z(1)
         for gj in range(2):
-            for half in range(2):
-                turn_a(0, gj, half)
-        group_p(1, 0, "scalar")
-        load_p(2, 1)
-        quant_x(0, 0)
-        quant_a(0, 0)
+            turn_a(0, gj, 0)
+        for k in range(6, 7):
+            make_offset(k, "scalar")
         new_x(0, 1)
+        for k in range(7, 9):
+            make_offset(k, "vector")
         x_vector(0, 1, 0)
-        quant_a(0, 1)
-        x_vector(0, 1, 1)
-        x_vector(0, 1, 2)
-        quant_p(1, 0)
-        x_vector(0, 1, 3)
+        group_x(0, 0)
         for gj in range(2):
-            for half in range(2):
-                turn_a(1, gj, half)
+            turn_a(0, gj, 1)
+        group_p(1, 0, "scalar", 0, 2)
+        x_vector(0, 1, 1)
+        quant_x(0, 0)
+        for gj in range(2):
+            turn_a(1, gj, 0)
+        group_p(1, 0, "scalar", 2, 4)
+        quant_a(0, 0)
+        quant_a(0, 1)
+        x_vector(0, 1, 2)
+        for gj in range(2):
+            turn_a(1, gj, 1)
+        for k in range(9, 10):
+            make_offset(k, "scalar")
         group_p(1, 1, "scalar")
         group_p(2, 0, "scalar")
-        quant_a(1, 0)
-        quant_x(0, 1)
+        for k in range(10, 12):
+            make_offset(k, "vector")
+        x_vector(0, 1, 3)
+        quant_p(1, 0)
         v_part(0, 0)
+        quant_a(1, 0)
         quant_a(1, 1)
         v_part(0, 1)
+        quant_x(0, 1)
         v_part(0, 2)
         v_part(0, 3)
         v_part(1, 0)
@@ -374,9 +408,9 @@ def tile_merged_dlinear_style_forecast_k4_kernel(
         v_part(1, 3)
         for t in range(4):
             x_scalar(1, 0, t)
-        quant_p(2, 0)
-        quant_v(1)
         group_p(2, 1, "scalar")
+        quant_v(1)
+        quant_p(2, 0)
         for t in range(2):
             x_scalar(1, 1, t)
         y_part(0, 0)
@@ -395,8 +429,6 @@ def tile_merged_dlinear_style_forecast_k4_kernel(
         for t in range(4):
             x_scalar(2, 1, t)
         group_y(0, 0)
-        for k in range(9, 12):
-            make_offset(k, "scalar")
         quant_x(1, 1)
         group_x(2, 0)
         y_part(1, 0)

@@ -114,7 +114,7 @@ def tile_merged_dlinear_style_forecast_k4_kernel(
 
         def group_p(G, g, engine, u0=0, u1=PACK, base=0, width=KP):
             if (G, g) not in p_grp:
-                p_grp[G, g] = sb("p_grp%d%d" % (G, g), [P, KP, PACK], BF16, tag="grp", bufs=10)
+                p_grp[G, g] = sb("p_grp%d%d" % (G, g), [P, KP, PACK], BF16, tag="grp", bufs=7)
             out = p_grp[G, g][:, base : base + width, :].rearrange("p (u n i) j -> p n u i j", u=PACK, i=2)
             out = out[:, :, u0:u1]
             in_ = p_raw[G, g, base].rearrange("p j (n i u) -> p n u i j", u=PACK, i=2)[:, :, u0:u1]
@@ -157,15 +157,18 @@ def tile_merged_dlinear_style_forecast_k4_kernel(
                 )
 
         def new_x(G, gl):
-            x_grp[G, gl] = sb("x_grp%d%d" % (G, gl), [P, KP, PACK], BF16, tag="grp", bufs=10)
+            if G == 0:
+                x_grp[G, gl] = sb("x_grp%d%d" % (G, gl), [P, KP, PACK], BF16, tag="grp", bufs=7)
+            else:
+                x_grp[G, gl] = sb("x_grp%d%d" % (G, gl), [P, KP, PACK], BF16, tag="x_late%d" % G, bufs=1)
 
         def x_vector(G, gl, cc):
             acc = bank("xv%d%d%d" % (G, gl, cc), [P, PACK, P])
             for t in range(PACK):
                 x_matmul(acc[:, t, :], G, gl, t, slice(cc * P, (cc + 1) * P))
-            out = x_grp[G, gl][:, cc * P : (cc + 1) * P, :]
-            g4 = gain[:, gl, :].unsqueeze(1).to_broadcast([P, P, PACK])
-            nc.vector.tensor_tensor(out=out, in0=acc[:].rearrange("p t c -> p c t"), in1=g4, op=ALU.mult)
+            out = x_grp[G, gl][:, cc * P : (cc + 1) * P, :].rearrange("p (c i) t -> p c t i", i=2)
+            g4 = gain[:, gl, :].unsqueeze(1).unsqueeze(3).to_broadcast([P, P // 2, PACK, 2])
+            nc.vector.tensor_tensor(out=out, in0=acc[:].rearrange("p t (c i) -> p c t i", i=2), in1=g4, op=ALU.mult)
 
         opened = {}
 
@@ -175,7 +178,7 @@ def tile_merged_dlinear_style_forecast_k4_kernel(
 
         def x_scalar(G, gl, t):
             if t == 0:
-                x_slots[G, gl] = sb("x_slots%d%d" % (G, gl), [P, PACK, KP], BF16, tag="x_slots", bufs=2)
+                x_slots[G, gl] = sb("x_slots%d%d" % (G, gl), [P, PACK, KP], BF16, tag="x_slots", bufs=3)
             if (G, gl, t) in opened:
                 acc = opened[G, gl, t]
                 x_matmul(acc[:], G, gl, t, slice(0, KP), (1,))
@@ -186,9 +189,17 @@ def tile_merged_dlinear_style_forecast_k4_kernel(
                 out=x_slots[G, gl][:, t, :], in_=acc[:], func=ACT.Copy, scale=gain[:, gl, t : t + 1],
             )
 
-        def group_x(G, gl):
+        def group_x(G, gl, split=KP):
             new_x(G, gl)
-            interleave("vector", x_grp[G, gl], x_slots[G, gl], 0, KP)
+            if G > 0 and gl == 1:
+                nc.gpsimd.tensor_scalar(
+                    out=x_grp[G, gl][:, 0:split, :], in0=x_slots[G, gl][:, :, 0:split].rearrange("p t c -> p c t"),
+                    scalar1=1.0, scalar2=0.0, op0=ALU.mult, op1=ALU.add,
+                )
+                if split < KP:
+                    interleave("scalar", x_grp[G, gl], x_slots[G, gl], split, KP)
+            else:
+                interleave("vector", x_grp[G, gl], x_slots[G, gl], 0, KP)
 
         def quant_x(G, gl):
             x_codes[G, gl] = sb("x_codes%d%d" % (G, gl), [P, KP], U32)
@@ -197,7 +208,10 @@ def tile_merged_dlinear_style_forecast_k4_kernel(
 
         def turn_a(gl, gj, half):
             if half == 0:
-                a_grp[gl, gj] = sb("a_grp%d%d" % (gl, gj), [P, KP, PACK], BF16, tag="grp", bufs=10)
+                if (gl, gj) == (1, 1):
+                    a_grp[gl, gj] = sb("a_grp_last", [P, KP, PACK], BF16)
+                else:
+                    a_grp[gl, gj] = sb("a_grp%d%d" % (gl, gj), [P, KP, PACK], BF16, tag="grp", bufs=7)
             acc = bank("at%d%d%d" % (gl, gj, half), [P, 2, 2, P])
             words = a_raw[gl, half][:].bitcast(F32)
             for u in range(2):
@@ -215,7 +229,7 @@ def tile_merged_dlinear_style_forecast_k4_kernel(
 
         def v_part(gl, hc):
             if hc == 0:
-                v_grp[gl] = sb("v_grp%d" % gl, [P, H, PACK], BF16, tag="grp", bufs=10)
+                v_grp[gl] = sb("v_grp%d" % gl, [P, H, PACK], BF16)
             acc = bank("v%d%d" % (gl, hc), [P, PACK, P])
             for t in range(PACK):
                 for gj in range(2):
@@ -229,9 +243,9 @@ def tile_merged_dlinear_style_forecast_k4_kernel(
                         stop=(gj == 1),
                     )
             nc.vector.tensor_tensor(
-                out=v_grp[gl][:, hc * P : (hc + 1) * P, :].rearrange("p (c i) t -> p c t i", i=RUN),
-                in0=acc[:].rearrange("p t (c i) -> p c t i", i=RUN),
-                in1=r_raw[gl][:, :, hc * P : (hc + 1) * P].rearrange("p t (c i) -> p c t i", i=RUN),
+                out=v_grp[gl][:, hc * P : (hc + 1) * P, :].rearrange("p (c i) t -> p c t i", i=2),
+                in0=acc[:].rearrange("p t (c i) -> p c t i", i=2),
+                in1=r_raw[gl][:, :, hc * P : (hc + 1) * P].rearrange("p t (c i) -> p c t i", i=2),
                 op=ALU.add,
             )
 
@@ -240,9 +254,9 @@ def tile_merged_dlinear_style_forecast_k4_kernel(
             v_scales[gl] = sb("v_scales%d" % gl, [P, H], U8)
             quantize(v_codes[gl][:], v_scales[gl][:], v_grp[gl][:])
 
-        def make_offset(k, engine):
+        def make_offset(k, engine, after=None):
             G, u = divmod(k, PACK)
-            offset[G, u] = sb("offset%d%d" % (G, u), [P, H], F32)
+            offset[G, u] = sb("offset%d%d" % (G, u), [P, H], F32, tag=after)
             if engine == "scalar":
                 nc.scalar.activation(
                     out=offset[G, u][:], in_=hb_all[:], func=ACT.Identity,
@@ -279,7 +293,7 @@ def tile_merged_dlinear_style_forecast_k4_kernel(
             nc.sync.dma_start(out=dst[:, lo:hi, :], in_=y32[G][:, lo:hi, :])
 
         def group_y(G, split):
-            y_grp[G] = sb("y_grp%d" % G, [P, H, PACK], BF16, tag="grp", bufs=10)
+            y_grp[G] = sb("y_grp%d" % G, [P, H, PACK], BF16, tag="grp", bufs=7)
             if split < H:
                 interleave("scalar", y_grp[G], y32[G], split, H)
             if split > 0:
@@ -329,18 +343,18 @@ def tile_merged_dlinear_style_forecast_k4_kernel(
         load_p(0, 1)
         load_z(0, 1, 2)
         load_ch()
-        load_a(0, 0)
         load_z(1)
+        load_a(0, 0)
         load_a(0, 1)
         load_p(1, 0)
         load_a(1, 0)
-        load_a(1, 1)
         load_d()
-        load_r(0)
+        load_a(1, 1)
         load_p(1, 1)
-        load_r(1)
+        load_r(0)
         load_p(2, 0)
         load_p(2, 1)
+        load_r(1)
         order_zs()
         gain_bank = consts_gain()
         group_p(0, 0, "scalar", 3, PACK)
@@ -358,89 +372,80 @@ def tile_merged_dlinear_style_forecast_k4_kernel(
         quant_p(0, 1)
         for k in range(0, 2):
             make_offset(k, "scalar")
+        order_z(1)
+        make_offset(2, "gpsimd", "z_raw10")
+        for k in range(3, 6):
+            make_offset(k, "gpsimd")
         for t in range(4):
             x_scalar(0, 0, t)
-        for k in range(2, 6):
-            make_offset(k, "vector")
-        order_z(1)
+        new_x(0, 1)
+        x_vector(0, 1, 0)
         for gj in range(2):
             turn_a(0, gj, 0)
-        for k in range(6, 7):
-            make_offset(k, "scalar")
-        new_x(0, 1)
-        for k in range(7, 9):
-            make_offset(k, "vector")
-        x_vector(0, 1, 0)
+        x_vector(0, 1, 1)
         group_x(0, 0)
         for gj in range(2):
             turn_a(0, gj, 1)
         group_p(1, 0, "scalar", 0, 2)
-        x_vector(0, 1, 1)
+        x_vector(0, 1, 2)
         quant_x(0, 0)
         for gj in range(2):
             turn_a(1, gj, 0)
-        group_p(1, 0, "scalar", 2, 4)
         quant_a(0, 0)
         quant_a(0, 1)
-        x_vector(0, 1, 2)
+        x_vector(0, 1, 3)
+        group_p(1, 0, "vector", 2, 4)
         for gj in range(2):
             turn_a(1, gj, 1)
-        for k in range(9, 10):
-            make_offset(k, "scalar")
         group_p(1, 1, "scalar")
         group_p(2, 0, "scalar")
-        for k in range(10, 12):
-            make_offset(k, "vector")
-        x_vector(0, 1, 3)
+        group_p(2, 1, "scalar")
         quant_p(1, 0)
-        v_part(0, 0)
         quant_a(1, 0)
-        quant_a(1, 1)
-        v_part(0, 1)
         quant_x(0, 1)
-        v_part(0, 2)
-        v_part(0, 3)
-        v_part(1, 0)
+        quant_a(1, 1)
+        make_offset(6, "gpsimd", "a_grp_last")
+        for k in range(7, 9):
+            make_offset(k, "gpsimd")
+        for hc in range(4):
+            v_part(0, hc)
         quant_p(1, 1)
-        v_part(1, 1)
         quant_v(0)
-        v_part(1, 2)
-        v_part(1, 3)
+        make_offset(9, "gpsimd", "v_grp0")
+        for k in range(10, 12):
+            make_offset(k, "gpsimd")
+        for hc in range(4):
+            v_part(1, hc)
         for t in range(4):
             x_scalar(1, 0, t)
-        group_p(2, 1, "scalar")
-        quant_v(1)
         quant_p(2, 0)
-        for t in range(2):
-            x_scalar(1, 1, t)
-        y_part(0, 0)
-        group_x(1, 0)
-        y_part(0, 1)
+        quant_v(1)
         quant_p(2, 1)
-        y_part(0, 2)
-        quant_x(1, 0)
-        y_part(0, 3)
-        store_y(0, 0, 4)
-        for t in range(2, 4):
-            x_scalar(1, 1, t)
         for t in range(4):
+            x_scalar(1, 1, t)
+        group_x(1, 0)
+        quant_x(1, 0)
+        group_x(1, 1, 416)
+        for u in range(2):
+            y_part(0, u)
+        for t in range(2):
             x_scalar(2, 0, t)
-        group_x(1, 1)
+        for u in range(2, 4):
+            y_part(0, u)
+        for t in range(2, 4):
+            x_scalar(2, 0, t)
+        store_y(0, 0, 4)
         for t in range(4):
             x_scalar(2, 1, t)
-        group_y(0, 0)
-        quant_x(1, 1)
         group_x(2, 0)
-        y_part(1, 0)
-        store_y(1, 0, 1)
+        quant_x(1, 1)
         quant_x(2, 0)
-        group_x(2, 1)
-        y_part(1, 1)
-        store_y(1, 1, 2)
-        quant_x(2, 1)
-        for u in range(2, 4):
+        group_x(2, 1, 416)
+        group_y(0, 0)
+        for u in range(4):
             y_part(1, u)
             store_y(1, u, u + 1)
+        quant_x(2, 1)
         quant_y(0)
         group_y(1, 0)
         for u in range(4):

from contextlib import ExitStack

import concourse.mybir as mybir
from concourse.masks import make_identity

S, C, L, H = 1024, 1536, 1024, 512
FLOPS = 2 * (S * C * L + L * L * H + C * L * H)

F32 = mybir.dt.float32
BF16 = mybir.dt.bfloat16
I32 = mybir.dt.int32
U32 = mybir.dt.uint32
U8 = mybir.dt.uint8
FP8X4 = mybir.dt.float8_e4m3fn_x4
FP4X4 = mybir.dt.float4_e2m1fn_x4
ALU = mybir.AluOpType
ACT = mybir.ActivationFunctionType

P = 128
PACK = 4
KP = P * PACK
NG = C // KP
RUN = 4


def tile_merged_dlinear_style_forecast_k4_kernel(
    tc, series_words, series_scales, mix, time_gain, avg, diff_words, diff_scales, w_rem, h_bias, ch_scale, ch_level,
    out_0, out_1, out_2,
):
    nc = tc.nc
    with ExitStack() as ctx:
        keep = ctx.enter_context(tc.tile_pool(name="keep", bufs=1))
        psum = ctx.enter_context(tc.psum_pool(name="psum", bufs=8))
        ctx.enter_context(tc.manual_schedule())

        def sb(name, shape, dtype, tag=None, bufs=1):
            return keep.tile(shape, dtype, name=name, tag=tag or name, bufs=bufs, align_bytes=64)

        def bank(name, shape, dtype=F32):
            return psum.tile(shape, dtype, name=name, tag="bank")

        def interleave(engine, dst, src, lo, hi):
            out = dst[:, lo:hi, :].rearrange("p (c i) t -> p c t i", i=RUN)
            in_ = src[:, :, lo:hi].rearrange("p t (c i) -> p c t i", i=RUN)
            if engine == "vector":
                nc.vector.tensor_copy(out=out, in_=in_)
            else:
                nc.scalar.copy(out=out, in_=in_)

        def quantize(codes, scales, grouped):
            nc.vector.quantize_mx(out=codes.bitcast(FP8X4), scales=scales, in_=grouped.rearrange("p c t -> p (c t)"))

        ident = sb("ident", [P, P], F32)
        ident_bf = sb("ident_bf", [P, P], BF16)
        zs_raw = sb("zs_raw", [P, L], U8)
        zs = sb("zs", [P, L], U8)
        ds = sb("ds", [P, 2, H], U8)
        dw = sb("dw", [P, 2, 2 * H], U8)
        gain_raw = sb("gain_raw", [2, KP], BF16)
        gain_rows = sb("gain_rows", [P, KP], BF16)
        gain = sb("gain", [P, 2, PACK], F32)
        hb_words = sb("hb_words", [P, PACK], BF16)
        hb_all = sb("hb_all", [P, H], BF16)
        ch_raw = sb("ch_raw", [P, 2, 16], BF16)
        ch = sb("ch", [P, 2, NG * PACK], F32)
        y_scales = sb("y_scales", [P, NG, H], U8)

        p_raw, p_grp, p_codes, p_scales = {}, {}, {}, {}
        z_raw, z_codes = {}, {}
        a_raw, a_grp, a_codes, a_scales = {}, {}, {}, {}
        r_raw, v_grp, v_codes, v_scales = {}, {}, {}, {}
        x_slots, x_grp, x_codes, x_scales = {}, {}, {}, {}
        offset, y32, y_grp, y_codes = {}, {}, {}, {}

        def load_p(G, g, lo=0, hi=KP):
            raw = sb("p_raw%d%d_%d" % (G, g, lo), [P, PACK, hi - lo], BF16)
            src = mix[g * KP : (g + 1) * KP, G * KP + lo : G * KP + hi].rearrange("(p j) c -> p j c", j=PACK)
            nc.sync.dma_start(out=raw[:], in_=src)
            if hi - lo <= KP:
                p_raw[G, g, lo] = raw[:]
            else:
                for i in range((hi - lo) // KP):
                    p_raw[G + i, g, 0] = raw[:, :, i * KP : (i + 1) * KP]

        def load_z(gl, g0=0, g1=2):
            z_raw[gl, g0] = sb("z_raw%d%d" % (gl, g0), [P, g1 - g0, KP], U32)
            src = series_words.rearrange("g p n t -> p g (n t)")[:, g0:g1, gl * KP * 4 : (gl + 1) * KP * 4].bitcast(I32)
            nc.sync.dma_start(out=z_raw[gl, g0][:].bitcast(I32), in_=src)

        def load_plane(queue, plane, rows):
            for q in range(4):
                src = rows[:, 4 * q : 4 * q + 4, :].rearrange("g r n -> r g n").bitcast(I32)
                queue.dma_start(out=plane[32 * q : 32 * q + 4, :, :].bitcast(I32), in_=src)

        def load_zs():
            for q in range(4):
                src = series_scales[:, 4 * q : 4 * q + 4, :].bitcast(I32)
                nc.sync.dma_start(out=zs_raw[32 * q : 32 * q + 8, :].bitcast(I32), in_=src)

        def load_a(gl, half):
            a_raw[gl, half] = sb("a_raw%d%d" % (gl, half), [P, 2, L], BF16)
            src = avg[gl * KP : (gl + 1) * KP, :].rearrange("(p a) j -> p a j", a=RUN)
            nc.sync.dma_start(out=a_raw[gl, half][:], in_=src[:, 2 * half : 2 * half + 2, :])

        def load_d():
            load_plane(nc.sync, ds, diff_scales)
            nc.sync.dma_start(out=dw[:].bitcast(I32), in_=diff_words.rearrange("g p n -> p g n").bitcast(I32))

        def load_r(gl):
            r_raw[gl] = sb("r_raw%d" % gl, [P, PACK, H], BF16)
            rows = w_rem[gl * KP : (gl + 1) * KP, :].rearrange("(m t r) h -> r m t h", t=PACK, r=RUN)
            for r in range(RUN):
                nc.sync.dma_start(out=r_raw[gl][r:P:RUN, :, :], in_=rows[r])

        def group_p(G, g, engine, u0=0, u1=PACK, base=0, width=KP):
            if (G, g) not in p_grp:
                p_grp[G, g] = sb("p_grp%d%d" % (G, g), [P, KP, PACK], BF16, tag="grp", bufs=7)
            out = p_grp[G, g][:, base : base + width, :].rearrange("p (u n i) j -> p n u i j", u=PACK, i=2)
            out = out[:, :, u0:u1]
            in_ = p_raw[G, g, base].rearrange("p j (n i u) -> p n u i j", u=PACK, i=2)[:, :, u0:u1]
            if engine == "vector":
                nc.vector.tensor_copy(out=out, in_=in_)
            else:
                nc.scalar.copy(out=out, in_=in_)

        def quant_p(G, g, lo=0, hi=KP):
            if lo == 0:
                p_codes[G, g] = sb("p_codes%d%d" % (G, g), [P, KP], U32)
                p_scales[G, g] = sb("p_scales%d%d" % (G, g), [P, KP], U8)
            quantize(p_codes[G, g][:, lo:hi], p_scales[G, g][:, lo:hi], p_grp[G, g][:, lo:hi, :])

        def order_z(gl, g0=0, g1=2):
            codes = sb("z_codes%d%d" % (gl, g0), [P, g1 - g0, KP], U32)
            nc.vector.tensor_copy(
                out=codes[:].bitcast(I32).rearrange("p g (t m r) -> p g t m r", t=PACK, r=RUN),
                in_=z_raw[gl, g0][:].bitcast(I32).rearrange("p g (m t r) -> p g t m r", t=PACK, r=RUN),
            )
            for g in range(g0, g1):
                z_codes[gl, g] = codes[:, g - g0, :]

        def order_zs():
            nc.vector.tensor_copy(
                out=zs[:].bitcast(I32).rearrange("p (g t m) -> p g t m", t=PACK, m=P // RUN),
                in_=zs_raw[:].bitcast(I32).rearrange("p (g m t) -> p g t m", t=PACK, m=P // RUN),
            )

        def x_matmul(out, G, gl, t, cols, passes=(0, 1)):
            for g in passes:
                nc.tensor.matmul_mx(
                    out=out,
                    lhsT=z_codes[gl, g][:, t * P : (t + 1) * P].bitcast(FP8X4),
                    lhsT_scale=zs[4 * g : P, gl * KP + t * P : gl * KP + (t + 1) * P],
                    rhs=p_codes[G, g][:, cols].bitcast(FP8X4),
                    rhs_scale=p_scales[G, g][:, cols],
                    start=(g == 0),
                    stop=(g == 1),
                )

        def new_x(G, gl):
            if G == 0:
                x_grp[G, gl] = sb("x_grp%d%d" % (G, gl), [P, KP, PACK], BF16, tag="grp", bufs=7)
            else:
                x_grp[G, gl] = sb("x_grp%d%d" % (G, gl), [P, KP, PACK], BF16, tag="x_late%d" % G, bufs=1)

        def x_vector(G, gl, cc):
            acc = bank("xv%d%d%d" % (G, gl, cc), [P, PACK, P])
            for t in range(PACK):
                x_matmul(acc[:, t, :], G, gl, t, slice(cc * P, (cc + 1) * P))
            out = x_grp[G, gl][:, cc * P : (cc + 1) * P, :].rearrange("p (c i) t -> p c t i", i=2)
            g4 = gain[:, gl, :].unsqueeze(1).unsqueeze(3).to_broadcast([P, P // 2, PACK, 2])
            nc.vector.tensor_tensor(out=out, in0=acc[:].rearrange("p t (c i) -> p c t i", i=2), in1=g4, op=ALU.mult)

        opened = {}

        def x_open(G, gl, t):
            opened[G, gl, t] = bank("xs%d%d%d" % (G, gl, t), [P, KP])
            x_matmul(opened[G, gl, t][:], G, gl, t, slice(0, KP), (0,))

        def x_scalar(G, gl, t):
            if t == 0:
                x_slots[G, gl] = sb("x_slots%d%d" % (G, gl), [P, PACK, KP], BF16, tag="x_slots", bufs=3)
            if (G, gl, t) in opened:
                acc = opened[G, gl, t]
                x_matmul(acc[:], G, gl, t, slice(0, KP), (1,))
            else:
                acc = bank("xs%d%d%d" % (G, gl, t), [P, KP])
                x_matmul(acc[:], G, gl, t, slice(0, KP))
            nc.scalar.activation(
                out=x_slots[G, gl][:, t, :], in_=acc[:], func=ACT.Copy, scale=gain[:, gl, t : t + 1],
            )

        def group_x(G, gl, split=KP):
            new_x(G, gl)
            if G > 0 and gl == 1:
                nc.gpsimd.tensor_scalar(
                    out=x_grp[G, gl][:, 0:split, :], in0=x_slots[G, gl][:, :, 0:split].rearrange("p t c -> p c t"),
                    scalar1=1.0, scalar2=0.0, op0=ALU.mult, op1=ALU.add,
                )
                if split < KP:
                    interleave("scalar", x_grp[G, gl], x_slots[G, gl], split, KP)
            else:
                interleave("vector", x_grp[G, gl], x_slots[G, gl], 0, KP)

        def quant_x(G, gl):
            x_codes[G, gl] = sb("x_codes%d%d" % (G, gl), [P, KP], U32)
            x_scales[G, gl] = sb("x_scales%d%d" % (G, gl), [P, KP], U8)
            quantize(x_codes[G, gl][:], x_scales[G, gl][:], x_grp[G, gl][:])

        def turn_a(gl, gj, half):
            if half == 0:
                if (gl, gj) == (1, 1):
                    a_grp[gl, gj] = sb("a_grp_last", [P, KP, PACK], BF16)
                else:
                    a_grp[gl, gj] = sb("a_grp%d%d" % (gl, gj), [P, KP, PACK], BF16, tag="grp", bufs=7)
            acc = bank("at%d%d%d" % (gl, gj, half), [P, 2, 2, P])
            words = a_raw[gl, half][:].bitcast(F32)
            for u in range(2):
                for a in range(2):
                    nc.tensor.transpose(acc[:, u, a, :], words[:, a, 2 * P * gj + u : 2 * P * (gj + 1) : 2], ident[:])
            out = a_grp[gl, gj][:].rearrange("p c t -> p (c t)").bitcast(F32)
            out = out.rearrange("p (t m r u) -> p m t r u", t=PACK, r=RUN, u=2)[:, :, :, 2 * half : 2 * half + 2, :]
            in_ = acc[:].rearrange("p u r (m t) -> p m t r u", t=PACK)
            nc.scalar.copy(out=out, in_=in_)

        def quant_a(gl, gj):
            a_codes[gl, gj] = sb("a_codes%d%d" % (gl, gj), [P, KP], U32)
            a_scales[gl, gj] = sb("a_scales%d%d" % (gl, gj), [P, KP], U8)
            quantize(a_codes[gl, gj][:], a_scales[gl, gj][:], a_grp[gl, gj][:])

        def v_part(gl, hc):
            if hc == 0:
                v_grp[gl] = sb("v_grp%d" % gl, [P, H, PACK], BF16)
            acc = bank("v%d%d" % (gl, hc), [P, PACK, P])
            for t in range(PACK):
                for gj in range(2):
                    nc.tensor.matmul_mx(
                        out=acc[:, t, :],
                        lhsT=a_codes[gl, gj][:, t * P : (t + 1) * P].bitcast(FP8X4),
                        lhsT_scale=a_scales[gl, gj][:, t * P : (t + 1) * P],
                        rhs=dw[:, gj, 2 * hc * P : 2 * (hc + 1) * P].bitcast(FP4X4),
                        rhs_scale=ds[:, gj, hc * P : (hc + 1) * P],
                        start=(gj == 0),
                        stop=(gj == 1),
                    )
            nc.vector.tensor_tensor(
                out=v_grp[gl][:, hc * P : (hc + 1) * P, :].rearrange("p (c i) t -> p c t i", i=2),
                in0=acc[:].rearrange("p t (c i) -> p c t i", i=2),
                in1=r_raw[gl][:, :, hc * P : (hc + 1) * P].rearrange("p t (c i) -> p c t i", i=2),
                op=ALU.add,
            )

        def quant_v(gl):
            v_codes[gl] = sb("v_codes%d" % gl, [P, H], U32)
            v_scales[gl] = sb("v_scales%d" % gl, [P, H], U8)
            quantize(v_codes[gl][:], v_scales[gl][:], v_grp[gl][:])

        def make_offset(k, engine, after=None):
            G, u = divmod(k, PACK)
            offset[G, u] = sb("offset%d%d" % (G, u), [P, H], F32, tag=after)
            if engine == "scalar":
                nc.scalar.activation(
                    out=offset[G, u][:], in_=hb_all[:], func=ACT.Identity,
                    scale=ch[:, 0, k : k + 1], bias=ch[:, 1, k : k + 1],
                )
            else:
                (nc.vector if engine == "vector" else nc.gpsimd).tensor_scalar(
                    out=offset[G, u][:], in0=hb_all[:], scalar1=ch[:, 0, k : k + 1], scalar2=ch[:, 1, k : k + 1],
                    op0=ALU.mult, op1=ALU.add,
                )

        def y_part(G, u):
            if u == 0:
                y32[G] = sb("y32_%d" % G, [P, PACK, H], F32)
            acc = bank("y%d%d" % (G, u), [P, H])
            for gl in range(2):
                nc.tensor.matmul_mx(
                    out=acc[:],
                    lhsT=x_codes[G, gl][:, u * P : (u + 1) * P].bitcast(FP8X4),
                    lhsT_scale=x_scales[G, gl][:, u * P : (u + 1) * P],
                    rhs=v_codes[gl][:].bitcast(FP8X4),
                    rhs_scale=v_scales[gl][:],
                    start=(gl == 0),
                    stop=(gl == 1),
                )
            k = G * PACK + u
            nc.vector.scalar_tensor_tensor(
                out=y32[G][:, u, :], in0=acc[:], scalar=ch[:, 0, k : k + 1], in1=offset[G, u][:],
                op0=ALU.mult, op1=ALU.add,
            )

        def store_y(G, lo, hi):
            dst = out_0[G * KP : (G + 1) * KP, :].rearrange("(p t) h -> p t h", t=PACK)
            nc.sync.dma_start(out=dst[:, lo:hi, :], in_=y32[G][:, lo:hi, :])

        def group_y(G, split):
            y_grp[G] = sb("y_grp%d" % G, [P, H, PACK], BF16, tag="grp", bufs=7)
            if split < H:
                interleave("scalar", y_grp[G], y32[G], split, H)
            if split > 0:
                interleave("vector", y_grp[G], y32[G], 0, split)

        def quant_y(G):
            y_codes[G] = sb("y_codes%d" % G, [P, H], U32)
            quantize(y_codes[G][:], y_scales[:, G, :], y_grp[G][:])
            dst = out_1[G].rearrange("p m t -> p (m t)").bitcast(I32)
            nc.sync.dma_start(out=dst, in_=y_codes[G][:].bitcast(I32))

        def consts_gain():
            nc.scalar.copy(
                out=gain_rows[0:2, :].rearrange("g (t m r) -> g t m r", t=PACK, r=RUN),
                in_=gain_raw[:].rearrange("g (m t r) -> g t m r", t=PACK, r=RUN),
            )
            gain_bank = bank("gain_bank", [P, PACK, P], BF16)
            for t in range(PACK):
                nc.tensor.transpose(gain_bank[:, t, :], gain_rows[:, t * P : (t + 1) * P], ident_bf[:])
            return gain_bank

        def consts_hb():
            hb_bank = bank("hb_bank", [P, 2, P])
            for w in range(2):
                nc.tensor.transpose(hb_bank[:, w, :], hb_words[:].bitcast(F32)[:, w : w + 1].to_broadcast([P, P]), ident[:])
            nc.scalar.copy(
                out=hb_all[:].bitcast(F32).rearrange("p (n w) -> p n w", w=2), in_=hb_bank[:].rearrange("p w n -> p n w")
            )

        def load_ch():
            for i, vec in enumerate((ch_scale, ch_level)):
                nc.sync.dma_start(
                    out=ch_raw[:, i, 0 : NG * PACK].rearrange("p (g t) -> p g t", t=PACK),
                    in_=vec.rearrange("(g p t) -> p g t", p=P, t=PACK),
                )

        nc.vector.memset(zs_raw[:].bitcast(I32), 0)
        nc.vector.memset(gain_rows[:], 0.0)
        nc.vector.memset(ds[:].rearrange("p g n -> p (g n)").bitcast(I32), 0)
        make_identity(nc, ident[:])
        nc.gpsimd.dma_start(out=hb_words[:], in_=h_bias.rearrange("(p t) -> p t", t=PACK))
        nc.scalar.copy(out=ident_bf[:], in_=ident[:])
        load_p(0, 0)
        load_zs()
        nc.sync.dma_start(out=gain_raw[:], in_=time_gain.rearrange("(g l) -> g l", g=2))
        load_z(0, 0, 1)
        load_p(0, 1)
        load_z(0, 1, 2)
        load_ch()
        load_z(1)
        load_a(0, 0)
        load_a(0, 1)
        load_p(1, 0)
        load_a(1, 0)
        load_d()
        load_a(1, 1)
        load_p(1, 1)
        load_r(0)
        load_p(2, 0)
        load_p(2, 1)
        load_r(1)
        order_zs()
        gain_bank = consts_gain()
        group_p(0, 0, "scalar", 3, PACK)
        group_p(0, 0, "vector", 0, 3)
        consts_hb()
        order_z(0, 0, 1)
        quant_p(0, 0)
        nc.scalar.copy(out=gain[:], in_=gain_bank[:, :, 0:2].rearrange("p t g -> p g t"))
        for t in range(4):
            x_open(0, 0, t)
        group_p(0, 1, "scalar", 3, PACK)
        group_p(0, 1, "vector", 0, 3)
        nc.scalar.copy(out=ch[:], in_=ch_raw[:, :, 0 : NG * PACK])
        order_z(0, 1, 2)
        quant_p(0, 1)
        for k in range(0, 2):
            make_offset(k, "scalar")
        order_z(1)
        make_offset(2, "gpsimd", "z_raw10")
        for k in range(3, 6):
            make_offset(k, "gpsimd")
        for t in range(4):
            x_scalar(0, 0, t)
        new_x(0, 1)
        x_vector(0, 1, 0)
        for gj in range(2):
            turn_a(0, gj, 0)
        x_vector(0, 1, 1)
        group_x(0, 0)
        for gj in range(2):
            turn_a(0, gj, 1)
        group_p(1, 0, "scalar", 0, 2)
        x_vector(0, 1, 2)
        quant_x(0, 0)
        for gj in range(2):
            turn_a(1, gj, 0)
        quant_a(0, 0)
        quant_a(0, 1)
        x_vector(0, 1, 3)
        group_p(1, 0, "vector", 2, 4)
        for gj in range(2):
            turn_a(1, gj, 1)
        group_p(1, 1, "scalar")
        group_p(2, 0, "scalar")
        group_p(2, 1, "scalar")
        quant_p(1, 0)
        quant_a(1, 0)
        quant_x(0, 1)
        quant_a(1, 1)
        make_offset(6, "gpsimd", "a_grp_last")
        for k in range(7, 9):
            make_offset(k, "gpsimd")
        for hc in range(4):
            v_part(0, hc)
        quant_p(1, 1)
        quant_v(0)
        make_offset(9, "gpsimd", "v_grp0")
        for k in range(10, 12):
            make_offset(k, "gpsimd")
        for hc in range(4):
            v_part(1, hc)
        for t in range(4):
            x_scalar(1, 0, t)
        quant_p(2, 0)
        quant_v(1)
        quant_p(2, 1)
        for t in range(4):
            x_scalar(1, 1, t)
        group_x(1, 0)
        quant_x(1, 0)
        group_x(1, 1, 416)
        for u in range(2):
            y_part(0, u)
        for t in range(2):
            x_scalar(2, 0, t)
        for u in range(2, 4):
            y_part(0, u)
        for t in range(2, 4):
            x_scalar(2, 0, t)
        store_y(0, 0, 4)
        for t in range(4):
            x_scalar(2, 1, t)
        group_x(2, 0)
        quant_x(1, 1)
        quant_x(2, 0)
        group_x(2, 1, 416)
        group_y(0, 0)
        for u in range(4):
            y_part(1, u)
            store_y(1, u, u + 1)
        quant_x(2, 1)
        quant_y(0)
        group_y(1, 0)
        for u in range(4):
            y_part(2, u)
            store_y(2, u, u + 1)
        group_y(2, 352)
        quant_y(1)
        quant_y(2)
        for q in range(4):
            queue = nc.scalar if q % 2 == 0 else nc.sync
            queue.dma_start(
                out=out_2[:, 4 * q : 4 * q + 4, :].rearrange("g r m -> r g m").bitcast(I32),
                in_=y_scales[32 * q : 32 * q + 4, :, :].bitcast(I32),
            )
